import numpy as np
import ml_dtypes


def mxq(x, axis, fmt="e4m3"):
    dtype, down = {"e4m3": (ml_dtypes.float8_e4m3fn, 7), "e5m2": (ml_dtypes.float8_e5m2, 14)}[fmt]
    v = np.moveaxis(np.asarray(x, np.float32).astype(ml_dtypes.bfloat16).astype(np.float64), axis, -1)
    blocks = v.reshape(v.shape[:-1] + (-1, 32))
    amax = np.abs(blocks).max(-1, keepdims=True)
    byte = np.maximum(np.where(amax > 0, np.frexp(amax)[1] - 1 + 127, 0) - down, 1)
    scale = np.exp2(byte - 127.0)
    codes = (blocks / scale).astype(np.float32).astype(dtype).astype(np.float64)
    return np.moveaxis((codes * scale).reshape(v.shape), -1, axis)


WIDE = False


def mx_kscale(k):
    if not WIDE:
        return np.ones(k)
    levels = np.array([10, -10, 5, -5, 0])
    if k % 512:
        return np.exp2(np.random.permutation(np.resize(levels, k // 32))).repeat(32)
    a = np.empty((k // 512, 16))
    for p in range(k // 512):
        a[p, :8] = np.random.permutation(np.resize(levels, 8))
        for g in range(8):
            far = levels[np.abs(levels - a[p, g]) >= 10]
            a[p, g + 8] = far[np.random.randint(len(far))]
    return np.exp2(a.ravel()).repeat(32)


def f64(x):
    return np.asarray(x).astype(np.float64)


def striped(idx):
    return np.tile(idx.reshape(-1, 16).T, (8, 1)).astype(np.uint16)


def unstriped(offs):
    return offs[:16].T.reshape(-1).astype(np.int64)


E2M1 = np.array([0.0, 0.5, 1.0, 1.5, 2.0, 3.0, 4.0, 6.0, -0.0, -0.5, -1.0, -1.5, -2.0, -3.0, -4.0, -6.0])


def pack_weight(w, fmt):
    k, n = w.shape
    w = f64(np.asarray(w, np.float32).astype(ml_dtypes.bfloat16)).reshape(k // 32, 32, n)
    amax = np.abs(w).max(1)
    if fmt == "e4m3":
        byte = np.frexp(amax)[1] - 1 + 127 - 7
    else:
        mant, ex = np.frexp(amax / 6.0)
        byte = np.where(mant > 0.5, ex, ex - 1) + 127
    byte = np.clip(np.where(amax > 0, byte, 1), 1, 254)
    scaled = (w * np.exp2(127.0 - byte)[:, None, :]).reshape(k, n).astype(np.float32)
    by_word = np.ascontiguousarray(scaled.reshape(k // 512, 128, 4, n).transpose(0, 1, 3, 2))
    if fmt == "e4m3":
        words = by_word.astype(ml_dtypes.float8_e4m3fn).view(np.uint8)
    else:
        c = by_word.astype(ml_dtypes.float4_e2m1fn).view(np.uint8) & 0xF
        words = (c[..., 0::2] | (c[..., 1::2] << 4)).reshape(k // 512, 128, 2 * n)
    return np.ascontiguousarray(words), np.ascontiguousarray(byte.astype(np.uint8).reshape(k // 512, 16, n))


def unpack_weight(words, scales, fmt):
    g, _, n = scales.shape
    words = np.ascontiguousarray(words).reshape(g, 128, n, -1)
    if fmt == "e4m3":
        vals = words.view(ml_dtypes.float8_e4m3fn).astype(np.float64)
    else:
        nib = np.empty((g, 128, n, 4), np.uint8)
        nib[..., 0::2] = words & 0xF
        nib[..., 1::2] = words >> 4
        vals = E2M1[nib]
    vals = vals * np.repeat(np.exp2(scales.astype(np.float64) - 127.0), 8, axis=1)[..., None]
    return vals.transpose(0, 1, 3, 2).reshape(g * 512, n)


def gelu(v):
    return 0.5 * v * (1.0 + np.tanh(np.sqrt(2.0 / np.pi) * (v + 0.044715 * v**3)))


K, H, N, T, S, P = 512, 1536, 768, 4096, 1024, 512

def setup_inputs():
    n = np.random.standard_normal
    s = mx_kscale(K)[:, None]
    u = mx_kscale(H)[:, None]
    tab_words, tab_scales = pack_weight(n((K, T)) * s, "e4m3")
    w2_words, w2_scales = pack_weight(n((K, H)) / np.sqrt(K) / s, "e2m1")
    wb_words, wb_scales = pack_weight(n((H, N)) / np.sqrt(H) / u, "e4m3")
    return {
        "tab_words": tab_words, "tab_scales": tab_scales,
        "offs": striped(np.random.permutation(T)[:S]),
        "pos1": striped(np.random.permutation(S)[:P]),
        "pos2": striped(np.random.permutation(S)[:P]),
        "w1": (n((K, H)) / np.sqrt(K) / s).astype(np.float32),
        "w2_words": w2_words, "w2_scales": w2_scales,
        "b2": (0.5 * n(H)).astype(np.float32),
        "gain": (np.exp(0.3 * n(H)) * u[:, 0]).astype(np.float32),
        "bs": (0.7 * n(H) * u[:, 0]).astype(np.float32),
        "wa": (n((H, N)) / np.sqrt(H) / u).astype(np.float32),
        "wb_words": wb_words, "wb_scales": wb_scales,
        "mt": n((N, P)).astype(np.float32),
    }

def reference(tab_words, tab_scales, offs, pos1, pos2, w1, w2_words, w2_scales,
              b2, gain, bs, wa, wb_words, wb_scales, mt):
    v = unpack_weight(tab_words, tab_scales, "e4m3")[:, unstriped(offs)]
    w2 = unpack_weight(w2_words, w2_scales, "e2m1")
    wb = unpack_weight(wb_words, wb_scales, "e4m3")
    e1 = mxq(f64(w1), 0, "e4m3").T @ v
    e2 = (w2.T @ v) + f64(b2)[:, None]
    h = np.minimum(e1, e2) * f64(gain)[:, None]
    xa = np.abs(h[:, unstriped(pos1)])
    xb = h[:, unstriped(pos2)] + f64(bs)[:, None]
    ya = mxq(f64(wa), 0, "e4m3").T @ mxq(xa, 0, "e4m3")
    yb = wb.T @ mxq(xb, 0, "e4m3")
    return ya * f64(mt) + yb

@@ -1,0 +1,315 @@
+from contextlib import ExitStack
+
+import concourse.mybir as mybir
+
+K, H, N, T, S, M = 512, 1536, 768, 4096, 1024, 512
+FLOPS = 2 * (2 * K * H * S + 2 * H * N * M)
+
+F32 = mybir.dt.float32
+BF16 = mybir.dt.bfloat16
+I32 = mybir.dt.int32
+U32 = mybir.dt.uint32
+U16 = mybir.dt.uint16
+U8 = mybir.dt.uint8
+FP8X4 = mybir.dt.float8_e4m3fn_x4
+FP4X4 = mybir.dt.float4_e2m1fn_x4
+ACT = mybir.ActivationFunctionType
+ALU = mybir.AluOpType
+
+P = 128
+PACK = 4
+KP = P * PACK
+BLOCKS = H // KP
+TILES = H // P
+BANK = 512
+HALF = M // 2
+WA_COLS = N // 2
+PAIRS = N // (2 * P)
+
+
+def tile_list_endotoxin_well_readout_kernel(
+    tc, tab_words, tab_scales, offs, pos1, pos2, w1, w2_words, w2_scales, b2, gain, bs, wa, wb_words, wb_scales, mt, out
+):
+    nc = tc.nc
+    with ExitStack() as ctx:
+        lists = ctx.enter_context(tc.tile_pool(name="lists", bufs=1))
+        keep = ctx.enter_context(tc.tile_pool(name="keep", bufs=1))
+        reuse = ctx.enter_context(tc.tile_pool(name="reuse", bufs=1))
+        ring = ctx.enter_context(tc.tile_pool(name="ring", bufs=2))
+        psum = ctx.enter_context(tc.psum_pool(name="psum", bufs=1))
+
+        wb_at = 0
+        mt_at = BLOCKS * N * 4
+        w1_at = mt_at - 4096
+        table_at = mt_at + (N // P) * M * 4
+
+        offs_t = lists.tile([P, S // 16], U16, name="offs_t")
+        pos1_t = lists.tile([P, M // 16], U16, name="pos1_t")
+        pos2_t = lists.tile([P, M // 16], U16, name="pos2_t")
+
+        def load_w1(b):
+            raw = reuse.tile([P, PACK, KP], F32, name="w1_raw", tag="w1_raw", offset=w1_at)
+            nc.sync.dma_start(out=raw[:], in_=w1[:, b * KP : (b + 1) * KP].rearrange("(p j) c -> p j c", j=PACK))
+            return raw
+
+        def load_scale_rows(queues, tile, rows):
+            for q in range(4):
+                queues[q].dma_start(out=tile[32 * q : 32 * q + 4].bitcast(I32), in_=rows(q).bitcast(I32))
+
+        def load_rows(queue, vec, name):
+            tile = keep.tile([P, BLOCKS, PACK], F32, name=name)
+            queue.dma_start(out=tile[:], in_=vec.rearrange("(b p t) -> p b t", p=P, t=PACK))
+            return tile[:].rearrange("p b t -> p (b t)")
+
+        nc.sync.dma_start(offs_t[:], offs)
+        nc.sync.dma_start(pos1_t[:], pos1)
+        nc.sync.dma_start(pos2_t[:], pos2)
+        w2_raw = keep.tile([P, H // 2], I32, name="w2_raw")
+        nc.sync.dma_start(out=w2_raw[:], in_=w2_words[0].bitcast(I32))
+        w1_raw0 = load_w1(0)
+        table = reuse.tile([P, T], U32, name="table", tag="table", offset=table_at)
+        nc.sync.dma_start(out=table[:].bitcast(I32), in_=tab_words[0].rearrange("p t i -> p (t i)").bitcast(I32))
+
+        gain_t = load_rows(nc.gpsimd, gain, "gain_t")
+        b2_t = load_rows(nc.gpsimd, b2, "b2_t")
+        bs_t = load_rows(nc.gpsimd, bs, "bs_t")
+        table_sc = keep.tile([P, T], U8, name="table_sc")
+        nc.vector.memset(table_sc[:].bitcast(I32), 0)
+        load_scale_rows([nc.scalar] * 4, table_sc, lambda q: tab_scales[0, 4 * q : 4 * q + 4, :])
+        w2_sc_raw = keep.tile([P, H], U8, name="w2_sc_raw")
+        nc.vector.memset(w2_sc_raw[:].bitcast(I32), 0)
+        load_scale_rows([nc.scalar] * 3 + [nc.gpsimd], w2_sc_raw, lambda q: w2_scales[0, 4 * q : 4 * q + 4, :])
+        wb_sc = keep.tile([P, BLOCKS, N], U8, name="wb_sc", align_bytes=64)
+        nc.vector.memset(wb_sc[:].rearrange("p a n -> p (a n)").bitcast(I32), 0)
+        load_scale_rows([nc.gpsimd] * 4, wb_sc, lambda q: wb_scales[:, 4 * q : 4 * q + 4, :].rearrange("a r n -> r a n"))
+
+        def quantise(grouped, name):
+            cols = grouped.shape[1] // PACK
+            codes = keep.tile([P, cols], U32, name=name + "_codes", align_bytes=64)
+            scales = keep.tile([P, cols], U8, name=name + "_scales", align_bytes=64)
+            nc.vector.quantize_mx(out=codes[:].bitcast(FP8X4), scales=scales[:], in_=grouped)
+            return codes, scales
+
+        def grouped_tile(cols):
+            return ring.tile([P, cols * PACK], BF16, name="grouped", tag="grouped", bufs=3, align_bytes=64)
+
+        def interleave_views(grouped, planes):
+            return (
+                grouped[:].rearrange("p (c i t) -> p c t i", i=4, t=PACK),
+                planes[:].rearrange("p t (c i) -> p c t i", i=4),
+            )
+
+        def round_w1(raw):
+            grouped = grouped_tile(KP)
+            nc.scalar.copy(
+                out=grouped[:].rearrange("p (t m j) -> p m j t", t=PACK, j=PACK),
+                in_=raw[:].rearrange("p j (m t) -> p m j t", t=PACK),
+            )
+            return grouped
+
+        def round_wa(piece):
+            a, u = divmod(piece, 2)
+            raw = reuse.tile([P, PACK, WA_COLS], F32, name="wa_raw", tag="wa_raw", bufs=2, offset=table_at)
+            nc.sync.dma_start(
+                out=raw[:],
+                in_=wa[a * KP : (a + 1) * KP, u * WA_COLS : (u + 1) * WA_COLS].rearrange("(p j) n -> p j n", j=PACK),
+            )
+            grouped = grouped_tile(WA_COLS)
+            dst, src = interleave_views(grouped, raw)
+            nc.scalar.copy(out=dst, in_=src)
+            return grouped
+
+        w1_q = {}
+        w1_grouped = round_w1(w1_raw0)
+
+        w2_codes = keep.tile([P, 2 * H], U8, name="w2_codes", align_bytes=64)
+        nc.vector.tensor_copy(
+            out=w2_codes[:].bitcast(U16).rearrange("p (b t m) -> p b t m", b=BLOCKS, t=PACK),
+            in_=w2_raw[:].bitcast(U16).rearrange("p (b m t) -> p b t m", b=BLOCKS, t=PACK),
+        )
+        picked_sc = keep.tile([P, S], U8, name="picked_sc", align_bytes=64)
+        nc.vector.tensor_copy(picked_sc[:], table_sc[:].indirect(offs_t[:]))
+        w2_sc = keep.tile([P, H], U8, name="w2_sc", align_bytes=64)
+        nc.vector.tensor_copy(
+            out=w2_sc[:].rearrange("p (b t m) -> p b t m", b=BLOCKS, t=PACK),
+            in_=w2_sc_raw[:].rearrange("p (b m t) -> p b t m", b=BLOCKS, t=PACK),
+        )
+
+        w1_q[0] = quantise(w1_grouped[:], "w1_0")
+
+        gain_abs = keep.tile([P, TILES], F32, name="gain_abs")
+        gain_sign = keep.tile([P, TILES], F32, name="gain_sign")
+        b2_gain = keep.tile([P, TILES], F32, name="b2_gain")
+        nc.scalar.activation(out=gain_abs[:], in_=gain_t, func=ACT.Abs)
+        nc.scalar.activation(out=gain_sign[:], in_=gain_t, func=ACT.Sign)
+        nc.vector.tensor_tensor(out=b2_gain[:], in0=gain_abs[:], in1=b2_t, op=ALU.mult)
+
+        picked = []
+        for h in range(S // BANK):
+            words = keep.tile([P, BANK], U32, name="picked%d" % h, align_bytes=64)
+            nc.vector.tensor_copy(words[:], table[:].indirect(offs_t[:, h * BANK // 16 : (h + 1) * BANK // 16]))
+            picked.append(words)
+
+        windows = [keep.tile([P, S], F32, name="window%d" % i) for i in range(TILES)]
+
+        def first_stage(i):
+            b, t = divmod(i, PACK)
+            codes, scales = w1_q[b]
+            for h in range(S // BANK):
+                cols = slice(h * BANK, (h + 1) * BANK)
+                e2 = psum.tile([P, BANK], F32, name="e2", tag="short", bufs=3)
+                nc.tensor.matmul_mx(
+                    out=e2[:],
+                    lhsT=w2_codes[:, 2 * P * i : 2 * P * (i + 1)].bitcast(FP4X4),
+                    lhsT_scale=w2_sc[:, P * i : P * (i + 1)],
+                    rhs=picked[h][:].bitcast(FP8X4),
+                    rhs_scale=picked_sc[:, cols],
+                    start=True,
+                    stop=True,
+                )
+                e1 = psum.tile([P, BANK], F32, name="e1", tag="long", bufs=5)
+                nc.tensor.matmul_mx(
+                    out=e1[:],
+                    lhsT=codes[:, P * t : P * (t + 1)].bitcast(FP8X4),
+                    lhsT_scale=scales[:, P * t : P * (t + 1)],
+                    rhs=picked[h][:].bitcast(FP8X4),
+                    rhs_scale=picked_sc[:, cols],
+                    start=True,
+                    stop=True,
+                )
+                second = ring.tile([P, BANK], F32, name="second", tag="second", bufs=4)
+                nc.scalar.activation(
+                    out=second[:], in_=e2[:], func=ACT.Identity,
+                    bias=b2_gain[:, i : i + 1], scale=gain_abs[:, i : i + 1],
+                )
+                nc.vector.scalar_tensor_tensor(
+                    out=windows[i][:, cols], in0=e1[:], scalar=gain_abs[:, i : i + 1], in1=second[:],
+                    op0=ALU.mult, op1=ALU.min,
+                )
+
+        def planes_tile(cols):
+            return ring.tile([P, PACK, cols], F32, name="planes", tag="planes", bufs=2)
+
+        xa_q, wa_q = {}, {}
+        xa_planes = {}
+        pending = []
+
+        def flush():
+            for store, key, grouped, name in pending:
+                store[key] = quantise(grouped[:], name)
+            pending.clear()
+
+        def pick_samples(i):
+            b, t = divmod(i, PACK)
+            if t == 0:
+                xa_planes[b] = planes_tile(M)
+            nc.vector.tensor_copy(xa_planes[b][:, t, :], windows[i][:].indirect(pos1_t[:]))
+            if t == PACK - 1:
+                grouped = grouped_tile(M)
+                dst, src = interleave_views(grouped, xa_planes[b])
+                nc.scalar.activation(out=dst, in_=src, func=ACT.Abs)
+                pending.append((xa_q, b, grouped, "xa%d" % b))
+
+        wa_steps = {2: 0, 3: 1, 6: 2, 8: 3, 10: 4}
+        for i in range(TILES):
+            b, t = divmod(i, PACK)
+            first_stage(i)
+            flush()
+            if i > 0:
+                pick_samples(i - 1)
+            if t == 1 and b + 1 < BLOCKS:
+                pending.append((w1_q, b + 1, round_w1(load_w1(b + 1)), "w1_%d" % (b + 1)))
+            if i in wa_steps:
+                pending.append((wa_q, wa_steps[i], round_wa(wa_steps[i]), "wa%d" % wa_steps[i]))
+        pick_samples(TILES - 1)
+
+        wb_codes = reuse.tile([P, BLOCKS, N], U32, name="wb_codes", tag="wb_codes", offset=wb_at, align_bytes=64)
+        nc.sync.dma_start(out=wb_codes[:].bitcast(I32), in_=wb_words.rearrange("a p n i -> p a (n i)").bitcast(I32))
+        result = reuse.tile([P, N // P, M], F32, name="result", tag="result", offset=mt_at)
+        nc.sync.dma_start(out=result[:], in_=mt.rearrange("(k p) m -> p k m", p=P))
+
+        def pick_spiked(h, b):
+            planes = planes_tile(HALF)
+            shifted = ring.tile([P, PACK, HALF], BF16, name="shifted", tag="shifted", bufs=2)
+            for t in range(PACK):
+                i = b * PACK + t
+                nc.vector.tensor_copy(
+                    planes[:, t, :], windows[i][:].indirect(pos2_t[:, h * HALF // 16 : (h + 1) * HALF // 16])
+                )
+                nc.scalar.activation(
+                    out=shifted[:, t, :], in_=planes[:, t, :], func=ACT.Identity,
+                    bias=bs_t[:, i : i + 1], scale=gain_sign[:, i : i + 1],
+                )
+            grouped = grouped_tile(HALF)
+            dst, src = interleave_views(grouped, shifted)
+            nc.scalar.copy(out=dst, in_=src)
+            return grouped
+
+        def result_view(h, k):
+            return result[:, 2 * k : 2 * k + 2, h * HALF : (h + 1) * HALF]
+
+        def sample_product(h, k):
+            ya = psum.tile([P, 2, HALF], F32, name="ya", tag="short", bufs=3)
+            cols = slice(h * HALF, (h + 1) * HALF)
+            for e in range(2):
+                u, c = divmod((2 * k + e) * P, WA_COLS)
+                for a in range(BLOCKS):
+                    nc.tensor.matmul_mx(
+                        out=ya[:, e, :],
+                        lhsT=wa_q[2 * a + u][0][:, c : c + P].bitcast(FP8X4),
+                        lhsT_scale=wa_q[2 * a + u][1][:, c : c + P],
+                        rhs=xa_q[a][0][:, cols].bitcast(FP8X4),
+                        rhs_scale=xa_q[a][1][:, cols],
+                        start=(a == 0),
+                        stop=(a == BLOCKS - 1),
+                    )
+            nc.vector.tensor_tensor(out=result_view(h, k), in0=ya[:], in1=result_view(h, k), op=ALU.mult)
+
+        yb = {}
+
+        def spiked_passes(h, b, grouped):
+            codes, scales = quantise(grouped[:], "xb%d_%d" % (h, b))
+            for k in range(PAIRS):
+                if b == 0:
+                    yb[h, k] = psum.tile([P, 2, HALF], F32, name="yb", tag="long", bufs=5)
+                for e in range(2):
+                    cols = slice((2 * k + e) * P, (2 * k + e + 1) * P)
+                    nc.tensor.matmul_mx(
+                        out=yb[h, k][:, e, :],
+                        lhsT=wb_codes[:, b, cols].bitcast(FP8X4),
+                        lhsT_scale=wb_sc[:, b, cols],
+                        rhs=codes[:].bitcast(FP8X4),
+                        rhs_scale=scales[:],
+                        start=(b == 0 and e == 0),
+                        stop=(b == BLOCKS - 1 and e == 1),
+                    )
+
+        def finish(h, k):
+            nc.vector.tensor_tensor(out=result_view(h, k), in0=yb[h, k][:], in1=result_view(h, k), op=ALU.add)
+            nc.sync.dma_start(
+                out=out[2 * k * P : (2 * k + 2) * P, h * HALF : (h + 1) * HALF].rearrange("(e p) m -> p e m", p=P),
+                in_=result_view(h, k),
+            )
+
+        steps = [(h, b) for h in range(2) for b in range(BLOCKS)]
+        waiting = None
+        for n, (h, b) in enumerate(steps):
+            grouped = pick_spiked(h, b)
+            flush()
+            if n == 0:
+                pending.append((wa_q, 5, round_wa(5), "wa5"))
+            if waiting is not None:
+                spiked_passes(*waiting)
+            waiting = (h, b, grouped)
+            if n == 2:
+                for k in range(PAIRS):
+                    sample_product(0, k)
+            if n == 3:
+                for k in range(PAIRS):
+                    finish(0, k)
+            if n == 4:
+                for k in range(PAIRS):
+                    sample_product(1, k)
+        spiked_passes(*waiting)
+        for k in range(PAIRS):
+            finish(1, k)

@@ -42,6 +42,7 @@ def tile_list_endotoxin_well_readout_kernel(
         mt_at = BLOCKS * N * 4
         w1_at = mt_at - 4096
         table_at = mt_at + (N // P) * M * 4
+        picked_at = table_at + T * 4
 
         offs_t = lists.tile([P, S // 16], U16, name="offs_t")
         pos1_t = lists.tile([P, M // 16], U16, name="pos1_t")
@@ -64,21 +65,21 @@ def tile_list_endotoxin_well_readout_kernel(
         nc.sync.dma_start(offs_t[:], offs)
         nc.sync.dma_start(pos1_t[:], pos1)
         nc.sync.dma_start(pos2_t[:], pos2)
+        gain_t = load_rows(nc.sync, gain, "gain_t")
+        b2_t = load_rows(nc.sync, b2, "b2_t")
         w2_raw = keep.tile([P, H // 2], I32, name="w2_raw")
         nc.sync.dma_start(out=w2_raw[:], in_=w2_words[0].bitcast(I32))
         w1_raw0 = load_w1(0)
         table = reuse.tile([P, T], U32, name="table", tag="table", offset=table_at)
         nc.sync.dma_start(out=table[:].bitcast(I32), in_=tab_words[0].rearrange("p t i -> p (t i)").bitcast(I32))
 
-        gain_t = load_rows(nc.gpsimd, gain, "gain_t")
-        b2_t = load_rows(nc.gpsimd, b2, "b2_t")
         bs_t = load_rows(nc.gpsimd, bs, "bs_t")
         table_sc = keep.tile([P, T], U8, name="table_sc")
         nc.vector.memset(table_sc[:].bitcast(I32), 0)
         load_scale_rows([nc.scalar] * 4, table_sc, lambda q: tab_scales[0, 4 * q : 4 * q + 4, :])
-        w2_sc_raw = keep.tile([P, H], U8, name="w2_sc_raw")
+        w2_sc_raw = reuse.tile([P, H], U8, name="w2_sc_raw", tag="w2_sc_raw", offset=picked_at + BANK * 4 - H // 2)
         nc.vector.memset(w2_sc_raw[:].bitcast(I32), 0)
-        load_scale_rows([nc.scalar] * 3 + [nc.gpsimd], w2_sc_raw, lambda q: w2_scales[0, 4 * q : 4 * q + 4, :])
+        load_scale_rows([nc.scalar] * 2 + [nc.gpsimd] * 2, w2_sc_raw, lambda q: w2_scales[0, 4 * q : 4 * q + 4, :])
         wb_sc = keep.tile([P, BLOCKS, N], U8, name="wb_sc", align_bytes=64)
         nc.vector.memset(wb_sc[:].rearrange("p a n -> p (a n)").bitcast(I32), 0)
         load_scale_rows([nc.gpsimd] * 4, wb_sc, lambda q: wb_scales[:, 4 * q : 4 * q + 4, :].rearrange("a r n -> r a n"))
@@ -114,9 +115,13 @@ def tile_list_endotoxin_well_readout_kernel(
                 out=raw[:],
                 in_=wa[a * KP : (a + 1) * KP, u * WA_COLS : (u + 1) * WA_COLS].rearrange("(p j) n -> p j n", j=PACK),
             )
-            grouped = grouped_tile(WA_COLS)
-            dst, src = interleave_views(grouped, raw)
-            nc.scalar.copy(out=dst, in_=src)
+            grouped = ring.tile([P, WA_COLS * PACK], BF16, name="wa_grouped", tag="wa_grouped", bufs=2, align_bytes=64)
+            for c in range(0, WA_COLS, WA_COLS // 2):
+                nc.gpsimd.tensor_scalar(
+                    out=grouped[:].rearrange("p (n j) -> p n j", j=PACK)[:, c : c + WA_COLS // 2, :],
+                    in0=raw[:, :, c : c + WA_COLS // 2].rearrange("p j n -> p n j"),
+                    scalar1=1.0, scalar2=0.0, op0=ALU.mult, op1=ALU.add,
+                )
             return grouped
 
         w1_q = {}
@@ -146,7 +151,9 @@ def tile_list_endotoxin_well_readout_kernel(
 
         picked = []
         for h in range(S // BANK):
-            words = keep.tile([P, BANK], U32, name="picked%d" % h, align_bytes=64)
+            words = reuse.tile(
+                [P, BANK], U32, name="picked%d" % h, tag="picked%d" % h, align_bytes=64, offset=picked_at + h * BANK * 4
+            )
             nc.vector.tensor_copy(words[:], table[:].indirect(offs_t[:, h * BANK // 16 : (h + 1) * BANK // 16]))
             picked.append(words)
 
@@ -157,7 +164,7 @@ def tile_list_endotoxin_well_readout_kernel(
             codes, scales = w1_q[b]
             for h in range(S // BANK):
                 cols = slice(h * BANK, (h + 1) * BANK)
-                e2 = psum.tile([P, BANK], F32, name="e2", tag="short", bufs=3)
+                e2 = psum.tile([P, BANK], F32, name="e2", tag="short", bufs=2)
                 nc.tensor.matmul_mx(
                     out=e2[:],
                     lhsT=w2_codes[:, 2 * P * i : 2 * P * (i + 1)].bitcast(FP4X4),
@@ -167,7 +174,7 @@ def tile_list_endotoxin_well_readout_kernel(
                     start=True,
                     stop=True,
                 )
-                e1 = psum.tile([P, BANK], F32, name="e1", tag="long", bufs=5)
+                e1 = psum.tile([P, BANK], F32, name="e1", tag="long", bufs=6)
                 nc.tensor.matmul_mx(
                     out=e1[:],
                     lhsT=codes[:, P * t : P * (t + 1)].bitcast(FP8X4),
@@ -177,13 +184,18 @@ def tile_list_endotoxin_well_readout_kernel(
                     start=True,
                     stop=True,
                 )
-                second = ring.tile([P, BANK], F32, name="second", tag="second", bufs=4)
+                if h == 0 and i > 0:
+                    if (i - 1) % PACK == 0:
+                        xa_planes[(i - 1) // PACK] = planes_tile(M)
+                    second = xa_planes[(i - 1) // PACK][:, (i - 1) % PACK, :]
+                else:
+                    second = ring.tile([P, BANK], F32, name="second", tag="second", bufs=3)[:]
                 nc.scalar.activation(
-                    out=second[:], in_=e2[:], func=ACT.Identity,
+                    out=second, in_=e2[:], func=ACT.Identity,
                     bias=b2_gain[:, i : i + 1], scale=gain_abs[:, i : i + 1],
                 )
                 nc.vector.scalar_tensor_tensor(
-                    out=windows[i][:, cols], in0=e1[:], scalar=gain_abs[:, i : i + 1], in1=second[:],
+                    out=windows[i][:, cols], in0=e1[:], scalar=gain_abs[:, i : i + 1], in1=second,
                     op0=ALU.mult, op1=ALU.min,
                 )
 
@@ -201,8 +213,6 @@ def tile_list_endotoxin_well_readout_kernel(
 
         def pick_samples(i):
             b, t = divmod(i, PACK)
-            if t == 0:
-                xa_planes[b] = planes_tile(M)
             nc.vector.tensor_copy(xa_planes[b][:, t, :], windows[i][:].indirect(pos1_t[:]))
             if t == PACK - 1:
                 grouped = grouped_tile(M)
@@ -210,7 +220,7 @@ def tile_list_endotoxin_well_readout_kernel(
                 nc.scalar.activation(out=dst, in_=src, func=ACT.Abs)
                 pending.append((xa_q, b, grouped, "xa%d" % b))
 
-        wa_steps = {2: 0, 3: 1, 6: 2, 8: 3, 10: 4}
+        wa_steps = {2: 0, 3: 1, 6: 2, 7: 3, 9: 4, 10: 5}
         for i in range(TILES):
             b, t = divmod(i, PACK)
             first_stage(i)
@@ -228,19 +238,19 @@ def tile_list_endotoxin_well_readout_kernel(
         result = reuse.tile([P, N // P, M], F32, name="result", tag="result", offset=mt_at)
         nc.sync.dma_start(out=result[:], in_=mt.rearrange("(k p) m -> p k m", p=P))
 
-        def pick_spiked(h, b):
-            planes = planes_tile(HALF)
-            shifted = ring.tile([P, PACK, HALF], BF16, name="shifted", tag="shifted", bufs=2)
+        def pick_spiked(b, first, count):
+            planes = planes_tile(count)
+            shifted = ring.tile([P, PACK, count], BF16, name="shifted", tag="shifted", bufs=2)
             for t in range(PACK):
                 i = b * PACK + t
                 nc.vector.tensor_copy(
-                    planes[:, t, :], windows[i][:].indirect(pos2_t[:, h * HALF // 16 : (h + 1) * HALF // 16])
+                    planes[:, t, :], windows[i][:].indirect(pos2_t[:, first // 16 : (first + count) // 16])
                 )
                 nc.scalar.activation(
                     out=shifted[:, t, :], in_=planes[:, t, :], func=ACT.Identity,
                     bias=bs_t[:, i : i + 1], scale=gain_sign[:, i : i + 1],
                 )
-            grouped = grouped_tile(HALF)
+            grouped = grouped_tile(count)
             dst, src = interleave_views(grouped, shifted)
             nc.scalar.copy(out=dst, in_=src)
             return grouped
@@ -248,8 +258,10 @@ def tile_list_endotoxin_well_readout_kernel(
         def result_view(h, k):
             return result[:, 2 * k : 2 * k + 2, h * HALF : (h + 1) * HALF]
 
-        def sample_product(h, k):
-            ya = psum.tile([P, 2, HALF], F32, name="ya", tag="short", bufs=3)
+        scaled = {}
+
+        def sample_product(h, k, dst):
+            ya = psum.tile([P, 2, HALF], F32, name="ya", tag="short", bufs=2)
             cols = slice(h * HALF, (h + 1) * HALF)
             for e in range(2):
                 u, c = divmod((2 * k + e) * P, WA_COLS)
@@ -263,53 +275,55 @@ def tile_list_endotoxin_well_readout_kernel(
                         start=(a == 0),
                         stop=(a == BLOCKS - 1),
                     )
-            nc.vector.tensor_tensor(out=result_view(h, k), in0=ya[:], in1=result_view(h, k), op=ALU.mult)
+            nc.vector.tensor_tensor(out=dst, in0=ya[:], in1=result_view(h, k), op=ALU.mult)
+            scaled[h, k] = dst
 
         yb = {}
 
-        def spiked_passes(h, b, grouped):
-            codes, scales = quantise(grouped[:], "xb%d_%d" % (h, b))
-            for k in range(PAIRS):
-                if b == 0:
-                    yb[h, k] = psum.tile([P, 2, HALF], F32, name="yb", tag="long", bufs=5)
-                for e in range(2):
-                    cols = slice((2 * k + e) * P, (2 * k + e + 1) * P)
-                    nc.tensor.matmul_mx(
-                        out=yb[h, k][:, e, :],
-                        lhsT=wb_codes[:, b, cols].bitcast(FP8X4),
-                        lhsT_scale=wb_sc[:, b, cols],
-                        rhs=codes[:].bitcast(FP8X4),
-                        rhs_scale=scales[:],
-                        start=(b == 0 and e == 0),
-                        stop=(b == BLOCKS - 1 and e == 1),
-                    )
+        def spiked_passes(b, first, count, grouped):
+            codes, scales = quantise(grouped[:], "xb%d_%d" % (b, first))
+            for c in range(0, count, HALF):
+                h = (first + c) // HALF
+                for k in range(PAIRS):
+                    if b == 0:
+                        yb[h, k] = psum.tile([P, 2, HALF], F32, name="yb", tag="long", bufs=6)
+                    for e in range(2):
+                        cols = slice((2 * k + e) * P, (2 * k + e + 1) * P)
+                        nc.tensor.matmul_mx(
+                            out=yb[h, k][:, e, :],
+                            lhsT=wb_codes[:, b, cols].bitcast(FP8X4),
+                            lhsT_scale=wb_sc[:, b, cols],
+                            rhs=codes[:, c : c + HALF].bitcast(FP8X4),
+                            rhs_scale=scales[:, c : c + HALF],
+                            start=(b == 0 and e == 0),
+                            stop=(b == BLOCKS - 1 and e == 1),
+                        )
 
         def finish(h, k):
-            nc.vector.tensor_tensor(out=result_view(h, k), in0=yb[h, k][:], in1=result_view(h, k), op=ALU.add)
+            nc.vector.tensor_tensor(out=result_view(h, k), in0=yb[h, k][:], in1=scaled[h, k], op=ALU.add)
             nc.sync.dma_start(
                 out=out[2 * k * P : (2 * k + 2) * P, h * HALF : (h + 1) * HALF].rearrange("(e p) m -> p e m", p=P),
                 in_=result_view(h, k),
             )
 
-        steps = [(h, b) for h in range(2) for b in range(BLOCKS)]
-        waiting = None
-        for n, (h, b) in enumerate(steps):
-            grouped = pick_spiked(h, b)
-            flush()
-            if n == 0:
-                pending.append((wa_q, 5, round_wa(5), "wa5"))
-            if waiting is not None:
-                spiked_passes(*waiting)
-            waiting = (h, b, grouped)
-            if n == 2:
-                for k in range(PAIRS):
-                    sample_product(0, k)
-            if n == 3:
-                for k in range(PAIRS):
-                    finish(0, k)
-            if n == 4:
-                for k in range(PAIRS):
-                    sample_product(1, k)
-        spiked_passes(*waiting)
+        xb0 = pick_spiked(0, 0, M)
+        flush()
+        xb1 = pick_spiked(1, 0, M)
+        spiked_passes(0, 0, M, xb0)
+        xb2_low = pick_spiked(2, 0, HALF)
+        spiked_passes(1, 0, M, xb1)
+        for k in range(PAIRS):
+            sample_product(0, k, result_view(0, k))
+        xb2_high = pick_spiked(2, HALF, HALF)
+        spiked_passes(2, 0, HALF, xb2_low)
+        early = planes_tile(HALF)
+        late = planes_tile(HALF)
+        sample_product(1, 0, early[:, 0:2, :])
+        finish(0, 0)
+        finish(0, 1)
+        spiked_passes(2, HALF, HALF, xb2_high)
+        finish(0, 2)
+        sample_product(1, 1, late[:, 0:2, :])
+        sample_product(1, 2, late[:, 2:4, :])
         for k in range(PAIRS):
             finish(1, k)

from contextlib import ExitStack

import concourse.mybir as mybir

K, H, N, T, S, M = 512, 1536, 768, 4096, 1024, 512
FLOPS = 2 * (2 * K * H * S + 2 * H * N * M)

F32 = mybir.dt.float32
BF16 = mybir.dt.bfloat16
I32 = mybir.dt.int32
U32 = mybir.dt.uint32
U16 = mybir.dt.uint16
U8 = mybir.dt.uint8
FP8X4 = mybir.dt.float8_e4m3fn_x4
FP4X4 = mybir.dt.float4_e2m1fn_x4
ACT = mybir.ActivationFunctionType
ALU = mybir.AluOpType

P = 128
PACK = 4
KP = P * PACK
BLOCKS = H // KP
TILES = H // P
BANK = 512
HALF = M // 2
WA_COLS = N // 2
PAIRS = N // (2 * P)


def tile_list_endotoxin_well_readout_kernel(
    tc, tab_words, tab_scales, offs, pos1, pos2, w1, w2_words, w2_scales, b2, gain, bs, wa, wb_words, wb_scales, mt, out
):
    nc = tc.nc
    with ExitStack() as ctx:
        lists = ctx.enter_context(tc.tile_pool(name="lists", bufs=1))
        keep = ctx.enter_context(tc.tile_pool(name="keep", bufs=1))
        reuse = ctx.enter_context(tc.tile_pool(name="reuse", bufs=1))
        ring = ctx.enter_context(tc.tile_pool(name="ring", bufs=2))
        psum = ctx.enter_context(tc.psum_pool(name="psum", bufs=1))

        wb_at = 0
        mt_at = BLOCKS * N * 4
        w1_at = mt_at - 4096
        table_at = mt_at + (N // P) * M * 4
        picked_at = table_at + T * 4

        offs_t = lists.tile([P, S // 16], U16, name="offs_t")
        pos1_t = lists.tile([P, M // 16], U16, name="pos1_t")
        pos2_t = lists.tile([P, M // 16], U16, name="pos2_t")

        def load_w1(b):
            raw = reuse.tile([P, PACK, KP], F32, name="w1_raw", tag="w1_raw", offset=w1_at)
            nc.sync.dma_start(out=raw[:], in_=w1[:, b * KP : (b + 1) * KP].rearrange("(p j) c -> p j c", j=PACK))
            return raw

        def load_scale_rows(queues, tile, rows):
            for q in range(4):
                queues[q].dma_start(out=tile[32 * q : 32 * q + 4].bitcast(I32), in_=rows(q).bitcast(I32))

        def load_rows(queue, vec, name):
            tile = keep.tile([P, BLOCKS, PACK], F32, name=name)
            queue.dma_start(out=tile[:], in_=vec.rearrange("(b p t) -> p b t", p=P, t=PACK))
            return tile[:].rearrange("p b t -> p (b t)")

        nc.sync.dma_start(offs_t[:], offs)
        nc.sync.dma_start(pos1_t[:], pos1)
        nc.sync.dma_start(pos2_t[:], pos2)
        gain_t = load_rows(nc.sync, gain, "gain_t")
        b2_t = load_rows(nc.sync, b2, "b2_t")
        w2_raw = keep.tile([P, H // 2], I32, name="w2_raw")
        nc.sync.dma_start(out=w2_raw[:], in_=w2_words[0].bitcast(I32))
        w1_raw0 = load_w1(0)
        table = reuse.tile([P, T], U32, name="table", tag="table", offset=table_at)
        nc.sync.dma_start(out=table[:].bitcast(I32), in_=tab_words[0].rearrange("p t i -> p (t i)").bitcast(I32))

        bs_t = load_rows(nc.gpsimd, bs, "bs_t")
        table_sc = keep.tile([P, T], U8, name="table_sc")
        nc.vector.memset(table_sc[:].bitcast(I32), 0)
        load_scale_rows([nc.scalar] * 4, table_sc, lambda q: tab_scales[0, 4 * q : 4 * q + 4, :])
        w2_sc_raw = reuse.tile([P, H], U8, name="w2_sc_raw", tag="w2_sc_raw", offset=picked_at + BANK * 4 - H // 2)
        nc.vector.memset(w2_sc_raw[:].bitcast(I32), 0)
        load_scale_rows([nc.scalar] * 2 + [nc.gpsimd] * 2, w2_sc_raw, lambda q: w2_scales[0, 4 * q : 4 * q + 4, :])
        wb_sc = keep.tile([P, BLOCKS, N], U8, name="wb_sc", align_bytes=64)
        nc.vector.memset(wb_sc[:].rearrange("p a n -> p (a n)").bitcast(I32), 0)
        load_scale_rows([nc.gpsimd] * 4, wb_sc, lambda q: wb_scales[:, 4 * q : 4 * q + 4, :].rearrange("a r n -> r a n"))

        def quantise(grouped, name):
            cols = grouped.shape[1] // PACK
            codes = keep.tile([P, cols], U32, name=name + "_codes", align_bytes=64)
            scales = keep.tile([P, cols], U8, name=name + "_scales", align_bytes=64)
            nc.vector.quantize_mx(out=codes[:].bitcast(FP8X4), scales=scales[:], in_=grouped)
            return codes, scales

        def grouped_tile(cols):
            return ring.tile([P, cols * PACK], BF16, name="grouped", tag="grouped", bufs=3, align_bytes=64)

        def interleave_views(grouped, planes):
            return (
                grouped[:].rearrange("p (c i t) -> p c t i", i=4, t=PACK),
                planes[:].rearrange("p t (c i) -> p c t i", i=4),
            )

        def round_w1(raw):
            grouped = grouped_tile(KP)
            nc.scalar.copy(
                out=grouped[:].rearrange("p (t m j) -> p m j t", t=PACK, j=PACK),
                in_=raw[:].rearrange("p j (m t) -> p m j t", t=PACK),
            )
            return grouped

        def round_wa(piece):
            a, u = divmod(piece, 2)
            raw = reuse.tile([P, PACK, WA_COLS], F32, name="wa_raw", tag="wa_raw", bufs=2, offset=table_at)
            nc.sync.dma_start(
                out=raw[:],
                in_=wa[a * KP : (a + 1) * KP, u * WA_COLS : (u + 1) * WA_COLS].rearrange("(p j) n -> p j n", j=PACK),
            )
            grouped = ring.tile([P, WA_COLS * PACK], BF16, name="wa_grouped", tag="wa_grouped", bufs=2, align_bytes=64)
            for c in range(0, WA_COLS, WA_COLS // 2):
                nc.gpsimd.tensor_scalar(
                    out=grouped[:].rearrange("p (n j) -> p n j", j=PACK)[:, c : c + WA_COLS // 2, :],
                    in0=raw[:, :, c : c + WA_COLS // 2].rearrange("p j n -> p n j"),
                    scalar1=1.0, scalar2=0.0, op0=ALU.mult, op1=ALU.add,
                )
            return grouped

        w1_q = {}
        w1_grouped = round_w1(w1_raw0)

        w2_codes = keep.tile([P, 2 * H], U8, name="w2_codes", align_bytes=64)
        nc.vector.tensor_copy(
            out=w2_codes[:].bitcast(U16).rearrange("p (b t m) -> p b t m", b=BLOCKS, t=PACK),
            in_=w2_raw[:].bitcast(U16).rearrange("p (b m t) -> p b t m", b=BLOCKS, t=PACK),
        )
        picked_sc = keep.tile([P, S], U8, name="picked_sc", align_bytes=64)
        nc.vector.tensor_copy(picked_sc[:], table_sc[:].indirect(offs_t[:]))
        w2_sc = keep.tile([P, H], U8, name="w2_sc", align_bytes=64)
        nc.vector.tensor_copy(
            out=w2_sc[:].rearrange("p (b t m) -> p b t m", b=BLOCKS, t=PACK),
            in_=w2_sc_raw[:].rearrange("p (b m t) -> p b t m", b=BLOCKS, t=PACK),
        )

        w1_q[0] = quantise(w1_grouped[:], "w1_0")

        gain_abs = keep.tile([P, TILES], F32, name="gain_abs")
        gain_sign = keep.tile([P, TILES], F32, name="gain_sign")
        b2_gain = keep.tile([P, TILES], F32, name="b2_gain")
        nc.scalar.activation(out=gain_abs[:], in_=gain_t, func=ACT.Abs)
        nc.scalar.activation(out=gain_sign[:], in_=gain_t, func=ACT.Sign)
        nc.vector.tensor_tensor(out=b2_gain[:], in0=gain_abs[:], in1=b2_t, op=ALU.mult)

        picked = []
        for h in range(S // BANK):
            words = reuse.tile(
                [P, BANK], U32, name="picked%d" % h, tag="picked%d" % h, align_bytes=64, offset=picked_at + h * BANK * 4
            )
            nc.vector.tensor_copy(words[:], table[:].indirect(offs_t[:, h * BANK // 16 : (h + 1) * BANK // 16]))
            picked.append(words)

        windows = [keep.tile([P, S], F32, name="window%d" % i) for i in range(TILES)]

        def first_stage(i):
            b, t = divmod(i, PACK)
            codes, scales = w1_q[b]
            for h in range(S // BANK):
                cols = slice(h * BANK, (h + 1) * BANK)
                e2 = psum.tile([P, BANK], F32, name="e2", tag="short", bufs=2)
                nc.tensor.matmul_mx(
                    out=e2[:],
                    lhsT=w2_codes[:, 2 * P * i : 2 * P * (i + 1)].bitcast(FP4X4),
                    lhsT_scale=w2_sc[:, P * i : P * (i + 1)],
                    rhs=picked[h][:].bitcast(FP8X4),
                    rhs_scale=picked_sc[:, cols],
                    start=True,
                    stop=True,
                )
                e1 = psum.tile([P, BANK], F32, name="e1", tag="long", bufs=6)
                nc.tensor.matmul_mx(
                    out=e1[:],
                    lhsT=codes[:, P * t : P * (t + 1)].bitcast(FP8X4),
                    lhsT_scale=scales[:, P * t : P * (t + 1)],
                    rhs=picked[h][:].bitcast(FP8X4),
                    rhs_scale=picked_sc[:, cols],
                    start=True,
                    stop=True,
                )
                if h == 0 and i > 0:
                    if (i - 1) % PACK == 0:
                        xa_planes[(i - 1) // PACK] = planes_tile(M)
                    second = xa_planes[(i - 1) // PACK][:, (i - 1) % PACK, :]
                else:
                    second = ring.tile([P, BANK], F32, name="second", tag="second", bufs=3)[:]
                nc.scalar.activation(
                    out=second, in_=e2[:], func=ACT.Identity,
                    bias=b2_gain[:, i : i + 1], scale=gain_abs[:, i : i + 1],
                )
                nc.vector.scalar_tensor_tensor(
                    out=windows[i][:, cols], in0=e1[:], scalar=gain_abs[:, i : i + 1], in1=second,
                    op0=ALU.mult, op1=ALU.min,
                )

        def planes_tile(cols):
            return ring.tile([P, PACK, cols], F32, name="planes", tag="planes", bufs=2)

        xa_q, wa_q = {}, {}
        xa_planes = {}
        pending = []

        def flush():
            for store, key, grouped, name in pending:
                store[key] = quantise(grouped[:], name)
            pending.clear()

        def pick_samples(i):
            b, t = divmod(i, PACK)
            nc.vector.tensor_copy(xa_planes[b][:, t, :], windows[i][:].indirect(pos1_t[:]))
            if t == PACK - 1:
                grouped = grouped_tile(M)
                dst, src = interleave_views(grouped, xa_planes[b])
                nc.scalar.activation(out=dst, in_=src, func=ACT.Abs)
                pending.append((xa_q, b, grouped, "xa%d" % b))

        wa_steps = {2: 0, 3: 1, 6: 2, 7: 3, 9: 4, 10: 5}
        for i in range(TILES):
            b, t = divmod(i, PACK)
            first_stage(i)
            flush()
            if i > 0:
                pick_samples(i - 1)
            if t == 1 and b + 1 < BLOCKS:
                pending.append((w1_q, b + 1, round_w1(load_w1(b + 1)), "w1_%d" % (b + 1)))
            if i in wa_steps:
                pending.append((wa_q, wa_steps[i], round_wa(wa_steps[i]), "wa%d" % wa_steps[i]))
        pick_samples(TILES - 1)

        wb_codes = reuse.tile([P, BLOCKS, N], U32, name="wb_codes", tag="wb_codes", offset=wb_at, align_bytes=64)
        nc.sync.dma_start(out=wb_codes[:].bitcast(I32), in_=wb_words.rearrange("a p n i -> p a (n i)").bitcast(I32))
        result = reuse.tile([P, N // P, M], F32, name="result", tag="result", offset=mt_at)
        nc.sync.dma_start(out=result[:], in_=mt.rearrange("(k p) m -> p k m", p=P))

        def pick_spiked(b, first, count):
            planes = planes_tile(count)
            shifted = ring.tile([P, PACK, count], BF16, name="shifted", tag="shifted", bufs=2)
            for t in range(PACK):
                i = b * PACK + t
                nc.vector.tensor_copy(
                    planes[:, t, :], windows[i][:].indirect(pos2_t[:, first // 16 : (first + count) // 16])
                )
                nc.scalar.activation(
                    out=shifted[:, t, :], in_=planes[:, t, :], func=ACT.Identity,
                    bias=bs_t[:, i : i + 1], scale=gain_sign[:, i : i + 1],
                )
            grouped = grouped_tile(count)
            dst, src = interleave_views(grouped, shifted)
            nc.scalar.copy(out=dst, in_=src)
            return grouped

        def result_view(h, k):
            return result[:, 2 * k : 2 * k + 2, h * HALF : (h + 1) * HALF]

        scaled = {}

        def sample_product(h, k, dst):
            ya = psum.tile([P, 2, HALF], F32, name="ya", tag="short", bufs=2)
            cols = slice(h * HALF, (h + 1) * HALF)
            for e in range(2):
                u, c = divmod((2 * k + e) * P, WA_COLS)
                for a in range(BLOCKS):
                    nc.tensor.matmul_mx(
                        out=ya[:, e, :],
                        lhsT=wa_q[2 * a + u][0][:, c : c + P].bitcast(FP8X4),
                        lhsT_scale=wa_q[2 * a + u][1][:, c : c + P],
                        rhs=xa_q[a][0][:, cols].bitcast(FP8X4),
                        rhs_scale=xa_q[a][1][:, cols],
                        start=(a == 0),
                        stop=(a == BLOCKS - 1),
                    )
            nc.vector.tensor_tensor(out=dst, in0=ya[:], in1=result_view(h, k), op=ALU.mult)
            scaled[h, k] = dst

        yb = {}

        def spiked_passes(b, first, count, grouped):
            codes, scales = quantise(grouped[:], "xb%d_%d" % (b, first))
            for c in range(0, count, HALF):
                h = (first + c) // HALF
                for k in range(PAIRS):
                    if b == 0:
                        yb[h, k] = psum.tile([P, 2, HALF], F32, name="yb", tag="long", bufs=6)
                    for e in range(2):
                        cols = slice((2 * k + e) * P, (2 * k + e + 1) * P)
                        nc.tensor.matmul_mx(
                            out=yb[h, k][:, e, :],
                            lhsT=wb_codes[:, b, cols].bitcast(FP8X4),
                            lhsT_scale=wb_sc[:, b, cols],
                            rhs=codes[:, c : c + HALF].bitcast(FP8X4),
                            rhs_scale=scales[:, c : c + HALF],
                            start=(b == 0 and e == 0),
                            stop=(b == BLOCKS - 1 and e == 1),
                        )

        def finish(h, k):
            nc.vector.tensor_tensor(out=result_view(h, k), in0=yb[h, k][:], in1=scaled[h, k], op=ALU.add)
            nc.sync.dma_start(
                out=out[2 * k * P : (2 * k + 2) * P, h * HALF : (h + 1) * HALF].rearrange("(e p) m -> p e m", p=P),
                in_=result_view(h, k),
            )

        xb0 = pick_spiked(0, 0, M)
        flush()
        xb1 = pick_spiked(1, 0, M)
        spiked_passes(0, 0, M, xb0)
        xb2_low = pick_spiked(2, 0, HALF)
        spiked_passes(1, 0, M, xb1)
        for k in range(PAIRS):
            sample_product(0, k, result_view(0, k))
        xb2_high = pick_spiked(2, HALF, HALF)
        spiked_passes(2, 0, HALF, xb2_low)
        early = planes_tile(HALF)
        late = planes_tile(HALF)
        sample_product(1, 0, early[:, 0:2, :])
        finish(0, 0)
        finish(0, 1)
        spiked_passes(2, HALF, HALF, xb2_high)
        finish(0, 2)
        sample_product(1, 1, late[:, 0:2, :])
        sample_product(1, 2, late[:, 2:4, :])
        for k in range(PAIRS):
            finish(1, k)
